import numpy as np
import ml_dtypes


def mxq(x, axis, fmt="e4m3"):
    dtype, down = {"e4m3": (ml_dtypes.float8_e4m3fn, 7), "e5m2": (ml_dtypes.float8_e5m2, 14)}[fmt]
    v = np.moveaxis(np.asarray(x, np.float32).astype(ml_dtypes.bfloat16).astype(np.float64), axis, -1)
    blocks = v.reshape(v.shape[:-1] + (-1, 32))
    amax = np.abs(blocks).max(-1, keepdims=True)
    byte = np.maximum(np.where(amax > 0, np.frexp(amax)[1] - 1 + 127, 0) - down, 1)
    scale = np.exp2(byte - 127.0)
    codes = (blocks / scale).astype(np.float32).astype(dtype).astype(np.float64)
    return np.moveaxis((codes * scale).reshape(v.shape), -1, axis)


WIDE = False


def mx_kscale(k):
    if not WIDE:
        return np.ones(k)
    levels = np.array([10, -10, 5, -5, 0])
    if k % 512:
        return np.exp2(np.random.permutation(np.resize(levels, k // 32))).repeat(32)
    a = np.empty((k // 512, 16))
    for p in range(k // 512):
        a[p, :8] = np.random.permutation(np.resize(levels, 8))
        for g in range(8):
            far = levels[np.abs(levels - a[p, g]) >= 10]
            a[p, g + 8] = far[np.random.randint(len(far))]
    return np.exp2(a.ravel()).repeat(32)


BF16 = ml_dtypes.bfloat16


def bf(x):
    return np.asarray(x, np.float32).astype(BF16)


def f64(x):
    return np.asarray(x).astype(np.float64)


E2M1 = np.array([0.0, 0.5, 1.0, 1.5, 2.0, 3.0, 4.0, 6.0, -0.0, -0.5, -1.0, -1.5, -2.0, -3.0, -4.0, -6.0])


def pack_weight(w, fmt):
    k, n = w.shape
    w = f64(bf(w)).reshape(k // 32, 32, n)
    amax = np.abs(w).max(1)
    if fmt == "e4m3":
        byte = np.frexp(amax)[1] - 1 + 127 - 7
    else:
        mant, ex = np.frexp(amax / 6.0)
        byte = np.where(mant > 0.5, ex, ex - 1) + 127
    byte = np.clip(np.where(amax > 0, byte, 1), 1, 254)
    scaled = (w * np.exp2(127.0 - byte)[:, None, :]).reshape(k, n).astype(np.float32)
    by_word = np.ascontiguousarray(scaled.reshape(k // 512, 128, 4, n).transpose(0, 1, 3, 2))
    if fmt == "e4m3":
        words = by_word.astype(ml_dtypes.float8_e4m3fn).view(np.uint8)
    else:
        c = by_word.astype(ml_dtypes.float4_e2m1fn).view(np.uint8) & 0xF
        words = c[..., 0::2] | (c[..., 1::2] << 4)
    return np.ascontiguousarray(words), np.ascontiguousarray(byte.astype(np.uint8).reshape(k // 512, 16, n))


def unpack_weight(words, scales, fmt):
    g, p, n, _ = words.shape
    if fmt == "e4m3":
        vals = np.ascontiguousarray(words).view(ml_dtypes.float8_e4m3fn).astype(np.float64)
    else:
        nib = np.empty((g, p, n, 4), np.uint8)
        nib[..., 0::2] = words & 0xF
        nib[..., 1::2] = words >> 4
        vals = E2M1[nib]
    vals = vals * np.repeat(np.exp2(scales.astype(np.float64) - 127.0), 8, axis=1)[..., None]
    return vals.transpose(0, 1, 3, 2).reshape(g * 512, n)
def pack4(w):
    words, scales = pack_weight(w, "e2m1")
    return words.reshape(words.shape[0], 128, -1), scales


def unpack4(words, scales):
    return unpack_weight(words.reshape(words.shape[0], 128, -1, 2), scales, "e2m1")


E4M3FN = np.array([(-1.0 if i & 128 else 1.0) * ((1.0 + (i & 7) / 8.0) * 2.0 ** (((i >> 3) & 15) - 7) if i & 120 else (i & 7) * 2.0 ** -9) for i in range(256)])


def e4m3fn_bytes(y):
    return np.clip(np.asarray(y, np.float64), -448.0, 448.0).astype(np.float32).astype(ml_dtypes.float8_e4m3fn).view(np.uint8)


def e4m3fn_values(b):
    return E4M3FN[b]

def planes(Y):
    n, m = Y.shape
    b = f64(bf(Y)).reshape(n // 32, 32, m)
    amax = np.abs(b).max(1)
    byte = np.clip(np.where(amax > 0, np.frexp(amax)[1] - 1 + 127 - 7, 1), 1, 254)
    codes = (b * np.exp2(127.0 - byte)[:, None, :]).reshape(n, m).astype(np.float32).astype(ml_dtypes.float8_e4m3fn).view(np.uint8)
    words = codes.reshape(n // 512, 128, 4, m).transpose(0, 1, 3, 2)
    return np.ascontiguousarray(words), np.ascontiguousarray(byte.astype(np.uint8).reshape(n // 512, 16, m))


T, D, R, F, N, B = 1024, 1024, 512, 1536, 512, 128
E4M3_MAX = 448.0
GELU_C = np.sqrt(2.0 / np.pi)

def setup_inputs():
    s, r, t = mx_kscale(D), mx_kscale(R), mx_kscale(F)
    X = np.random.randn(T, D) * s
    X_scale = (np.abs(X).reshape(T, D // B, B).max(axis=2) / E4M3_MAX).astype(np.float32)
    X_bytes = e4m3fn_bytes(X / np.repeat(f64(X_scale), B, axis=1))
    mem = np.random.randn(T, R) / r
    w_in = np.random.randn(D, F) / np.sqrt(D) / s[:, None]
    w_gate = np.random.randn(D, F) / np.sqrt(D) / s[:, None] * t
    w_mem_words, w_mem_scales = pack4(np.random.randn(R, F) / np.sqrt(R) * r[:, None])
    w_down = np.random.randn(F, N) / np.sqrt(F) / t[:, None]
    b_down = 0.4 * np.random.randn(1, N)
    slot_gain = np.exp(0.8 * np.random.randn(T, 1))
    return {"X_bytes": X_bytes, "X_scale": X_scale, "mem": bf(mem), "w_in": bf(w_in),
            "w_gate": bf(w_gate), "w_mem_words": w_mem_words, "w_mem_scales": w_mem_scales,
            "w_down": bf(w_down), "b_down": bf(b_down), "slot_gain": bf(slot_gain)}

def reference(X_bytes, X_scale, mem, w_in, w_gate, w_mem_words, w_mem_scales, w_down, b_down, slot_gain):
    X = e4m3fn_values(X_bytes) * np.repeat(f64(X_scale), B, axis=1)
    xq = mxq(X, 1, "e4m3")
    z = (xq @ mxq(f64(w_in), 0, "e4m3")) + (mxq(f64(mem), 1, "e4m3") @ unpack4(w_mem_words, w_mem_scales))
    u = xq @ mxq(f64(w_gate), 0, "e4m3")
    h = 0.5 * z * (1.0 + np.tanh(GELU_C * (z + 0.044715 * z * z * z))) * u
    y = ((mxq(h, 1, "e4m3") @ mxq(f64(w_down), 0, "e4m3")) + f64(b_down)) * f64(slot_gain)
    Y = y.reshape(T, N)
    words, scales = planes(Y)
    return y, words, scales

@@ -1,0 +1,394 @@
+from contextlib import ExitStack
+
+import concourse.mybir as mybir
+from concourse.masks import make_identity
+
+T, D, R, F, N = 1024, 1024, 512, 1536, 512
+FLOPS = 2 * T * (2 * D * F + R * F + F * N)
+
+F32 = mybir.dt.float32
+BF16 = mybir.dt.bfloat16
+I32 = mybir.dt.int32
+U32 = mybir.dt.uint32
+U8 = mybir.dt.uint8
+FP8 = mybir.dt.float8_e4m3fn
+FP8X4 = mybir.dt.float8_e4m3fn_x4
+FP4X4 = mybir.dt.float4_e2m1fn_x4
+ACT = mybir.ActivationFunctionType
+ALU = mybir.AluOpType
+
+P = 128
+PACK = 4
+KP = P * PACK
+TILES = T // P
+GROUPS = F // KP
+STEPS = GROUPS * TILES
+DOWN_FROM = 19
+
+
+def tile_gated_memory_expert_b10_kernel(
+    tc, X_bytes, X_scale, mem, w_in, w_gate, w_mem_words, w_mem_scales, w_down, b_down, slot_gain,
+    out_0, out_1, out_2,
+):
+    nc = tc.nc
+    with ExitStack() as ctx:
+        keep = ctx.enter_context(tc.tile_pool(name="keep", bufs=1))
+        stage = ctx.enter_context(tc.tile_pool(name="stage", bufs=3))
+        psum = ctx.enter_context(tc.psum_pool(name="psum", bufs=8))
+        ctx.enter_context(tc.manual_schedule())
+
+        def kept(name, shape, dtype):
+            return keep.tile(shape, dtype, name=name, align_bytes=64)
+
+        def staged(name, shape, dtype, bufs=3):
+            return stage.tile(shape, dtype, name=name, tag=name, bufs=bufs, align_bytes=64)
+
+        def bank():
+            return psum.tile([P, 512], F32, name="bank", tag="bank")
+
+        x_rows = X_bytes.rearrange("(h p t) k -> h p (t k)", p=P, t=PACK)
+        mem_rows = mem.rearrange("(h p t) k -> h p (t k)", p=P, t=PACK)
+        x_src, mem_src, raw = {}, {}, {}
+
+        def load_x(first, count):
+            half, t = divmod(first, PACK)
+            xb = kept("xbytes%d" % first, [P, count * D], U8)
+            nc.sync.dma_start(out=xb[:], in_=x_rows[half, :, t * D : (t + count) * D])
+            for n in range(count):
+                x_src[first + n] = xb[:, n * D : (n + 1) * D]
+
+        def load_mem(pair):
+            half, t = divmod(2 * pair, PACK)
+            mt = kept("mem%d" % pair, [P, 2 * R], BF16)
+            nc.sync.dma_start(out=mt[:], in_=mem_rows[half, :, t * R : (t + 2) * R])
+            mem_src[pair] = mt
+
+        def load_w(key):
+            which, g, c = key
+            rt = kept("raw_%s%d%d" % key, [P, PACK, KP], BF16)
+            if which == "down":
+                rows = w_down[g * KP : (g + 1) * KP, :].rearrange("(a t e) n -> e a t n", t=PACK, e=PACK)
+                for e in range(PACK):
+                    nc.sync.dma_start(out=rt[e:P:PACK, :, :], in_=rows[e])
+            else:
+                w = w_in if which == "in" else w_gate
+                rows = w[c * KP : (c + 1) * KP, g * KP : (g + 1) * KP]
+                nc.sync.dma_start(out=rt[:], in_=rows.rearrange("(p j) n -> p j n", j=PACK))
+            raw[key] = rt
+
+        wm_raw = {}
+
+        def load_wm(g0, g1):
+            wt = kept("wm_raw%d" % g0, [P, (g1 - g0) * 2 * KP], U8)
+            nc.sync.dma_start(out=wt[:].bitcast(I32), in_=w_mem_words[0, :, g0 * 2 * KP : g1 * 2 * KP].bitcast(I32))
+            wm_raw[g0] = wt
+
+        ident = kept("ident", [P, P], F32)
+        make_identity(nc, ident[:])
+        wms_raw = kept("wms_raw", [P, F], U8)
+        nc.vector.memset(wms_raw[:].bitcast(I32), 0)
+        for q in range(4):
+            nc.scalar.dma_start(
+                out=wms_raw[32 * q : 32 * q + 4, :].bitcast(I32), in_=w_mem_scales[0, 4 * q : 4 * q + 4, :].bitcast(I32)
+            )
+
+        warm = kept("warm", [P, 2], F32)
+        nc.vector.memset(warm[:, 0:1], 0.0)
+        nc.scalar.activation(out=warm[:, 1:2], in_=warm[:, 0:1], func=ACT.Gelu_apprx_tanh)
+
+        xs = kept("xs", [P, 2, PACK * 8], F32)
+        nc.sync.dma_start(out=xs[:], in_=X_scale.rearrange("(h p t) j -> p h (t j)", p=P, t=PACK))
+        load_x(0, 2)
+        load_w(("in", 0, 0))
+        load_w(("in", 0, 1))
+        load_mem(0)
+        load_wm(0, 1)
+        load_x(2, 2)
+        load_w(("gate", 0, 0))
+        load_w(("gate", 0, 1))
+        load_mem(1)
+        load_x(4, 4)
+        load_w(("in", 1, 0))
+        load_mem(2)
+        load_mem(3)
+        load_w(("in", 1, 1))
+        load_wm(1, 3)
+        later = [("in", 1, 0), ("in", 1, 1), ("gate", 1, 0), ("gate", 1, 1)]
+        later = later + [("in", 2, 0), ("in", 2, 1), ("gate", 2, 0), ("gate", 2, 1)]
+        later = later + [("down", g, 0) for g in range(GROUPS)]
+        for key in later[2:]:
+            load_w(key)
+        bias = kept("bias", [P, N], BF16)
+        nc.sync.dma_start(out=bias[:], in_=b_down.rearrange("o n -> (o n)").partition_broadcast(P))
+        gain_raw = kept("gain_raw", [P, 2, PACK], BF16)
+        nc.sync.dma_start(out=gain_raw[:], in_=slot_gain.rearrange("(h p t) o -> p h (t o)", p=P, t=PACK))
+        gain = kept("gain", [P, TILES], F32)
+
+        wide, turned, grouped, codes, scales = {}, {}, {}, {}, {}
+
+        def quantise(key):
+            src = grouped[key]
+            width = src.shape[1] // PACK
+            name = "%s%d%d" % key
+            codes[key] = kept("codes_" + name, [P, width], U32)
+            scales[key] = kept("scales_" + name, [P, width], U8)
+            nc.vector.quantize_mx(out=codes[key][:].bitcast(FP8X4), scales=scales[key][:], in_=src[:])
+
+        def widen(i):
+            half, t = divmod(i, PACK)
+            xw = staged("xw", [P, D], BF16, bufs=4)
+            dst = xw[:].rearrange("p (c u q r e) -> p c q r u e", c=2, u=2, q=4, e=2)
+            for b in range(8):
+                c, q = divmod(b, 4)
+                src = x_src[i][:, b * P : (b + 1) * P].bitcast(FP8).rearrange("p (r u e) -> p r u e", u=2, e=2)
+                nc.vector.tensor_scalar(
+                    out=dst[:, c, q, :, :, :], in0=src, scalar1=xs[:, half, t * 8 + b : t * 8 + b + 1], scalar2=None, op0=ALU.mult
+                )
+            wide[i] = xw
+
+        def turn_x(i):
+            words = wide[i][:].bitcast(F32)
+            pt = bank()
+            for n in range(4):
+                nc.tensor.transpose(pt[:, n * P : (n + 1) * P], words[:, n * P : (n + 1) * P], ident[:])
+            turned[("x", i, 0)] = pt
+
+        def turn_mem(pair):
+            words = mem_src[pair][:].bitcast(F32)
+            pt = bank()
+            for n in range(4):
+                c, u = divmod(n, 2)
+                nc.tensor.transpose(pt[:, n * P : (n + 1) * P], words[:, 256 * c + u : 256 * (c + 1) : 2], ident[:])
+            turned[("mem", pair, 0)] = pt
+
+        def empty(key):
+            gt = staged("act_grouped", [P, 1024], BF16, bufs=4)
+            nc.scalar.copy(
+                out=gt[:].bitcast(F32).rearrange("p (c r u) -> p c r u", c=2, u=2),
+                in_=turned[key][:].rearrange("p (c u r) -> p c r u", c=2, u=2),
+            )
+            grouped[key] = gt
+
+        def interleave(engine, key, t):
+            if t == 0:
+                grouped[key] = staged("w_grouped", [P, PACK * KP], BF16)
+            dst = grouped[key][:].rearrange("p (t a e j) -> p t a j e", t=4, e=4, j=4)[:, t, :, :, :]
+            order = "p j (t a e) -> p t a j e" if key[0] == "down" else "p j (a t e) -> p t a j e"
+            src = raw[key][:].rearrange(order, t=4, e=4)[:, t, :, :, :]
+            if engine == "vector":
+                nc.vector.tensor_copy(out=dst, in_=src)
+            else:
+                nc.scalar.copy(out=dst, in_=src)
+
+        wm = kept("wm", [P, GROUPS * 2 * KP], U8)
+        wms = kept("wms", [P, F], U8)
+
+        def sort_wm(g0, g1):
+            nc.vector.tensor_copy(
+                out=wm[:, g0 * 2 * KP : g1 * 2 * KP].bitcast(I32).rearrange("p (g t a w) -> p g t a w", t=4, a=32, w=2),
+                in_=wm_raw[g0][:].bitcast(I32).rearrange("p (g a t w) -> p g t a w", t=4, a=32, w=2),
+            )
+
+        def sort_wms():
+            nc.vector.tensor_copy(
+                out=wms[:].bitcast(I32).rearrange("p (g t a) -> p g t a", t=4, a=32),
+                in_=wms_raw[:].bitcast(I32).rearrange("p (g a t) -> p g t a", t=4, a=32),
+            )
+
+        def operand(key, first, count):
+            return codes[key][:, first : first + count].bitcast(FP8X4), scales[key][:, first : first + count]
+
+        z_bank, u_bank, act = {}, {}, {}
+
+        def first_stage(acc, which, s):
+            g, i = divmod(s, TILES)
+            for t in range(PACK):
+                out = acc[:, t * P : (t + 1) * P]
+                for c in range(2):
+                    wc, ws = operand((which, g, c), t * P, P)
+                    xc, xsc = operand(("x", i, 0), c * P, P)
+                    nc.tensor.matmul_mx(
+                        out=out, lhsT=wc, lhsT_scale=ws, rhs=xc, rhs_scale=xsc,
+                        start=(c == 0), stop=(c == 1 and which == "gate"),
+                    )
+                if which == "in":
+                    col = g * KP + t * P
+                    mc, ms = operand(("mem", i // 2, 0), (i % 2) * P, P)
+                    nc.tensor.matmul_mx(
+                        out=out, lhsT=wm[:, 2 * col : 2 * (col + P)].bitcast(FP4X4), lhsT_scale=wms[:, col : col + P],
+                        rhs=mc, rhs_scale=ms, start=False, stop=True,
+                    )
+
+        def sum_z(s):
+            z_bank[s] = bank()
+            first_stage(z_bank[s], "in", s)
+
+        def sum_u(s):
+            u_bank[s] = bank()
+            first_stage(u_bank[s], "gate", s)
+
+        def gelu(s):
+            act[s] = staged("gelu", [P, KP], F32)
+            nc.scalar.activation(
+                out=act[s][:].rearrange("p (r t) -> p r t", t=PACK),
+                in_=z_bank[s][:].rearrange("p (t r) -> p r t", t=PACK),
+                func=ACT.Gelu_apprx_tanh,
+            )
+
+        def gate(s):
+            h = staged("h_grouped", [P, KP], BF16)
+            nc.vector.tensor_tensor(
+                out=h[:].rearrange("p (r t) -> p r t", t=PACK),
+                in0=act[s][:].rearrange("p (r t) -> p r t", t=PACK),
+                in1=u_bank[s][:].rearrange("p (t r) -> p r t", t=PACK),
+                op=ALU.mult,
+            )
+            grouped[("h", s, 0)] = h
+
+        y = [kept("y%d" % h, [P, PACK, N], F32) for h in range(2)]
+        y_grouped = [kept("y_grouped%d" % h, [P, PACK * N], BF16) for h in range(2)]
+        y_codes = [kept("y_codes%d" % h, [P, N], U32) for h in range(2)]
+        y_scales = [kept("y_scales%d" % h, [P, N], U8) for h in range(2)]
+        y_rows = out_0.rearrange("(h p t) n -> h t p n", p=P, t=PACK)
+        y_bank = {}
+
+        def scale_bias(i):
+            nc.scalar.activation(out=y[i // PACK][:, i % PACK, :], in_=bias[:], func=ACT.Copy, scale=gain[:, i : i + 1])
+
+        def down(i):
+            y_bank[i] = bank()
+            for g in range(GROUPS):
+                hc, hs = operand(("h", g * TILES + i, 0), 0, P)
+                wc, ws = operand(("down", g, 0), 0, N)
+                nc.tensor.matmul_mx(
+                    out=y_bank[i][:], lhsT=hc, lhsT_scale=hs, rhs=wc, rhs_scale=ws, start=(g == 0), stop=(g == GROUPS - 1)
+                )
+
+        def finish(i):
+            half, t = divmod(i, PACK)
+            nc.vector.scalar_tensor_tensor(
+                out=y[half][:, t, :], in0=y_bank[i][:], scalar=gain[:, i : i + 1], in1=y[half][:, t, :],
+                op0=ALU.mult, op1=ALU.add,
+            )
+            nc.sync.dma_start(out=y_rows[half, t], in_=y[half][:, t, :])
+
+        def interleave_y(engine, half, c0, c1):
+            dst = y_grouped[half][:].rearrange("p (c e t) -> p c t e", e=4, t=4)[:, c0 // 4 : c1 // 4, :, :]
+            src = y[half][:].rearrange("p t (c e) -> p c t e", e=4)[:, c0 // 4 : c1 // 4, :, :]
+            if engine == "vector":
+                nc.vector.tensor_copy(out=dst, in_=src)
+            else:
+                nc.scalar.copy(out=dst, in_=src)
+
+        def quantise_y(half, c0, c1):
+            nc.vector.quantize_mx(
+                out=y_codes[half][:, c0:c1].bitcast(FP8X4), scales=y_scales[half][:, c0:c1],
+                in_=y_grouped[half][:, PACK * c0 : PACK * c1],
+            )
+            nc.sync.dma_start(
+                out=out_1[half].rearrange("p m t -> p (m t)")[:, PACK * c0 : PACK * c1].bitcast(I32),
+                in_=y_codes[half][:, c0:c1].bitcast(I32),
+            )
+
+        def store_scales(half, queues):
+            for q in range(4):
+                queues[q % len(queues)].dma_start(
+                    out=out_2[half, 4 * q : 4 * q + 4, :].bitcast(I32), in_=y_scales[half][32 * q : 32 * q + 4, :].bitcast(I32)
+                )
+
+        def share(key):
+            interleave("vector", key, 0)
+            interleave("vector", key, 1)
+            interleave("scalar", key, 2)
+            interleave("scalar", key, 3)
+
+        widen(0)
+        widen(1)
+        turn_x(0)
+        turn_x(1)
+        turn_mem(0)
+        empty(("x", 0, 0))
+        share(("in", 0, 0))
+        quantise(("x", 0, 0))
+        empty(("x", 1, 0))
+        share(("in", 0, 1))
+        quantise(("in", 0, 0))
+        empty(("mem", 0, 0))
+        sort_wm(0, 1)
+        sort_wms()
+        quantise(("x", 1, 0))
+        quantise(("in", 0, 1))
+        quantise(("mem", 0, 0))
+        widen(2)
+        share(("gate", 0, 0))
+        widen(3)
+        share(("gate", 0, 1))
+        quantise(("gate", 0, 0))
+        quantise(("gate", 0, 1))
+
+        quarters = [(key, t) for key in later for t in range(PACK)]
+        full = []
+        for s in range(STEPS):
+            ready, full = full, []
+            if s > 0:
+                gate(s - 1)
+            if s > DOWN_FROM:
+                finish(s - 1 - DOWN_FROM)
+            for key in ready:
+                quantise(key)
+            if 1 <= s and s + 1 < TILES:
+                quantise(("x", s + 1, 0))
+                if s % 2 == 1:
+                    quantise(("mem", (s + 1) // 2, 0))
+            sum_z(s)
+            gelu(s)
+            if s % 2 == 0 and s + 2 < TILES:
+                turn_x(s + 2)
+                turn_mem((s + 2) // 2)
+                turn_x(s + 3)
+            sum_u(s)
+            if s + 2 < TILES:
+                empty(("x", s + 2, 0))
+                if s % 2 == 0:
+                    empty(("mem", (s + 2) // 2, 0))
+            if s + 4 < TILES:
+                widen(s + 4)
+            if s == 5:
+                sort_wm(1, 3)
+            if s == 16:
+                nc.vector.tensor_copy(out=gain[:], in_=gain_raw[:].rearrange("p h t -> p (h t)"))
+            on_vector = 0 if s < 4 else (2 if s < TILES else 1)
+            on_scalar = 2 if s in (6, 7) or (s > TILES and s % 2 == 1) else 1
+            for engine, count in (("vector", on_vector), ("scalar", on_scalar)):
+                taken, quarters = quarters[:count], quarters[count:]
+                for key, t in taken:
+                    interleave(engine, key, t)
+                    if t == PACK - 1:
+                        full.append(key)
+            if s > 0:
+                quantise(("h", s - 1, 0))
+            if 18 <= s < 22:
+                scale_bias(2 * (s - 18))
+                scale_bias(2 * (s - 18) + 1)
+            if s >= DOWN_FROM:
+                down(s - DOWN_FROM)
+        last = STEPS - 1
+        interleave_y("scalar", 0, 0, 256)
+        interleave_y("scalar", 0, 256, 512)
+        gate(last)
+        finish(4)
+        down(5)
+        quantise(("h", last, 0))
+        finish(5)
+        down(6)
+        finish(6)
+        down(7)
+        quantise_y(0, 0, 512)
+        store_scales(0, [nc.sync])
+        finish(7)
+        interleave_y("scalar", 1, 384, 512)
+        interleave_y("vector", 1, 0, 256)
+        interleave_y("vector", 1, 256, 384)
+        quantise_y(1, 0, 256)
+        quantise_y(1, 256, 512)
+        store_scales(1, [nc.scalar, nc.sync])

@@ -22,8 +22,8 @@ PACK = 4
 KP = P * PACK
 TILES = T // P
 GROUPS = F // KP
-STEPS = GROUPS * TILES
-DOWN_FROM = 19
+BLOCKS = 2 * GROUPS
+GROUPED_BUFS = 5
 
 
 def tile_gated_memory_expert_b10_kernel(
@@ -87,30 +87,29 @@ def tile_gated_memory_expert_b10_kernel(
         make_identity(nc, ident[:])
         wms_raw = kept("wms_raw", [P, F], U8)
         nc.vector.memset(wms_raw[:].bitcast(I32), 0)
-        for q in range(4):
-            nc.scalar.dma_start(
-                out=wms_raw[32 * q : 32 * q + 4, :].bitcast(I32), in_=w_mem_scales[0, 4 * q : 4 * q + 4, :].bitcast(I32)
-            )
-
         warm = kept("warm", [P, 2], F32)
         nc.vector.memset(warm[:, 0:1], 0.0)
         nc.scalar.activation(out=warm[:, 1:2], in_=warm[:, 0:1], func=ACT.Gelu_apprx_tanh)
 
         xs = kept("xs", [P, 2, PACK * 8], F32)
-        nc.sync.dma_start(out=xs[:], in_=X_scale.rearrange("(h p t) j -> p h (t j)", p=P, t=PACK))
         load_x(0, 2)
-        load_w(("in", 0, 0))
-        load_w(("in", 0, 1))
-        load_mem(0)
-        load_wm(0, 1)
+        nc.sync.dma_start(out=xs[:], in_=X_scale.rearrange("(h p t) j -> p h (t j)", p=P, t=PACK))
         load_x(2, 2)
+        load_w(("in", 0, 0))
+        load_mem(0)
+        load_mem(1)
+        load_w(("in", 0, 1))
+        load_wm(0, 1)
+        for q in range(4):
+            nc.sync.dma_start(
+                out=wms_raw[32 * q : 32 * q + 4, :].bitcast(I32), in_=w_mem_scales[0, 4 * q : 4 * q + 4, :].bitcast(I32)
+            )
         load_w(("gate", 0, 0))
         load_w(("gate", 0, 1))
-        load_mem(1)
         load_x(4, 4)
-        load_w(("in", 1, 0))
         load_mem(2)
         load_mem(3)
+        load_w(("in", 1, 0))
         load_w(("in", 1, 1))
         load_wm(1, 3)
         later = [("in", 1, 0), ("in", 1, 1), ("gate", 1, 0), ("gate", 1, 1)]
@@ -134,44 +133,62 @@ def tile_gated_memory_expert_b10_kernel(
             scales[key] = kept("scales_" + name, [P, width], U8)
             nc.vector.quantize_mx(out=codes[key][:].bitcast(FP8X4), scales=scales[key][:], in_=src[:])
 
-        def widen(i):
-            half, t = divmod(i, PACK)
-            xw = staged("xw", [P, D], BF16, bufs=4)
-            dst = xw[:].rearrange("p (c u q r e) -> p c q r u e", c=2, u=2, q=4, e=2)
-            for b in range(8):
-                c, q = divmod(b, 4)
-                src = x_src[i][:, b * P : (b + 1) * P].bitcast(FP8).rearrange("p (r u e) -> p r u e", u=2, e=2)
-                nc.vector.tensor_scalar(
-                    out=dst[:, c, q, :, :, :], in0=src, scalar1=xs[:, half, t * 8 + b : t * 8 + b + 1], scalar2=None, op0=ALU.mult
-                )
-            wide[i] = xw
+        def fresh_grouped(key):
+            grouped[key] = staged("grouped", [P, PACK * KP], BF16, bufs=GROUPED_BUFS)
 
-        def turn_x(i):
-            words = wide[i][:].bitcast(F32)
+        def widen_plain(half, c, pair):
+            xw = staged("xw", [P, 2 * KP], BF16, bufs=4)
+            for n in range(2):
+                for q in range(4):
+                    t = 2 * pair + n
+                    b = 4 * c + q
+                    nc.scalar.activation(
+                        out=xw[:, n * KP + q * P : n * KP + (q + 1) * P], in_=x_src[PACK * half + t][:, b * P : (b + 1) * P].bitcast(FP8),
+                        func=ACT.Copy, scale=xs[:, half, t * 8 + b : t * 8 + b + 1],
+                    )
+            words = xw[:].bitcast(F32)
+            wide[(half, c, pair)] = [words[:, 256 * n + u : 256 * (n + 1) : 2] for n in range(2) for u in range(2)]
+
+        def widen(half, c, pair):
+            xw = staged("xw", [P, 2 * KP], BF16, bufs=4)
+            dst = xw[:].rearrange("p (n u q r e) -> p n q r u e", n=2, u=2, q=4, e=2)
+            for q in range(4):
+                for n in range(2):
+                    t = 2 * pair + n
+                    b = 4 * c + q
+                    src = x_src[PACK * half + t][:, b * P : (b + 1) * P].bitcast(FP8).rearrange("p (r u e) -> p r u e", u=2, e=2)
+                    nc.vector.tensor_scalar(
+                        out=dst[:, n, q, :, :, :], in0=src, scalar1=xs[:, half, t * 8 + b : t * 8 + b + 1], scalar2=None,
+                        op0=ALU.mult,
+                    )
+            words = xw[:].bitcast(F32)
+            wide[(half, c, pair)] = [words[:, n * P : (n + 1) * P] for n in range(4)]
+
+        def turn_x(half, c, pair):
             pt = bank()
             for n in range(4):
-                nc.tensor.transpose(pt[:, n * P : (n + 1) * P], words[:, n * P : (n + 1) * P], ident[:])
-            turned[("x", i, 0)] = pt
+                nc.tensor.transpose(pt[:, n * P : (n + 1) * P], wide[(half, c, pair)][n], ident[:])
+            turned[("x", half, c), pair] = pt
 
-        def turn_mem(pair):
-            words = mem_src[pair][:].bitcast(F32)
+        def turn_mem(half, pair):
+            words = mem_src[2 * half + pair][:].bitcast(F32)
             pt = bank()
             for n in range(4):
                 c, u = divmod(n, 2)
                 nc.tensor.transpose(pt[:, n * P : (n + 1) * P], words[:, 256 * c + u : 256 * (c + 1) : 2], ident[:])
-            turned[("mem", pair, 0)] = pt
+            turned[("mem", half, 0), pair] = pt
 
-        def empty(key):
-            gt = staged("act_grouped", [P, 1024], BF16, bufs=4)
+        def empty(key, pair):
+            if pair == 0:
+                fresh_grouped(key)
             nc.scalar.copy(
-                out=gt[:].bitcast(F32).rearrange("p (c r u) -> p c r u", c=2, u=2),
-                in_=turned[key][:].rearrange("p (c u r) -> p c r u", c=2, u=2),
+                out=grouped[key][:, pair * 2 * KP : (pair + 1) * 2 * KP].bitcast(F32).rearrange("p (c r u) -> p c r u", c=2, u=2),
+                in_=turned[key, pair][:].rearrange("p (c u r) -> p c r u", c=2, u=2),
             )
-            grouped[key] = gt
 
         def interleave(engine, key, t):
             if t == 0:
-                grouped[key] = staged("w_grouped", [P, PACK * KP], BF16)
+                fresh_grouped(key)
             dst = grouped[key][:].rearrange("p (t a e j) -> p t a j e", t=4, e=4, j=4)[:, t, :, :, :]
             order = "p j (t a e) -> p t a j e" if key[0] == "down" else "p j (a t e) -> p t a j e"
             src = raw[key][:].rearrange(order, t=4, e=4)[:, t, :, :, :]
@@ -200,50 +217,50 @@ def tile_gated_memory_expert_b10_kernel(
 
         z_bank, u_bank, act = {}, {}, {}
 
-        def first_stage(acc, which, s):
-            g, i = divmod(s, TILES)
+        def z_pass(b, t, which, start, stop):
+            g, half = divmod(b, 2)
+            if start:
+                z_bank[b, t] = bank()
+            if which == "mem":
+                col = g * KP + t * P
+                wc, ws = wm[:, 2 * col : 2 * (col + P)].bitcast(FP4X4), wms[:, col : col + P]
+                xc, xsc = operand(("mem", half, 0), 0, KP)
+            else:
+                wc, ws = operand(("in", g, which), t * P, P)
+                xc, xsc = operand(("x", half, which), 0, KP)
+            nc.tensor.matmul_mx(out=z_bank[b, t][:], lhsT=wc, lhsT_scale=ws, rhs=xc, rhs_scale=xsc, start=start, stop=stop)
+
+        def sum_z(b, t):
+            z_pass(b, t, 0, True, False)
+            z_pass(b, t, "mem", False, False)
+            z_pass(b, t, 1, False, True)
+
+        def sum_u(b, i):
+            g, half = divmod(b, 2)
+            u_bank[b, i] = bank()
             for t in range(PACK):
-                out = acc[:, t * P : (t + 1) * P]
                 for c in range(2):
-                    wc, ws = operand((which, g, c), t * P, P)
-                    xc, xsc = operand(("x", i, 0), c * P, P)
+                    wc, ws = operand(("gate", g, c), t * P, P)
+                    xc, xsc = operand(("x", half, c), i * P, P)
                     nc.tensor.matmul_mx(
-                        out=out, lhsT=wc, lhsT_scale=ws, rhs=xc, rhs_scale=xsc,
-                        start=(c == 0), stop=(c == 1 and which == "gate"),
-                    )
-                if which == "in":
-                    col = g * KP + t * P
-                    mc, ms = operand(("mem", i // 2, 0), (i % 2) * P, P)
-                    nc.tensor.matmul_mx(
-                        out=out, lhsT=wm[:, 2 * col : 2 * (col + P)].bitcast(FP4X4), lhsT_scale=wms[:, col : col + P],
-                        rhs=mc, rhs_scale=ms, start=False, stop=True,
+                        out=u_bank[b, i][:, t * P : (t + 1) * P], lhsT=wc, lhsT_scale=ws, rhs=xc, rhs_scale=xsc,
+                        start=(c == 0), stop=(c == 1),
                     )
 
-        def sum_z(s):
-            z_bank[s] = bank()
-            first_stage(z_bank[s], "in", s)
+        def gelu(b, t):
+            if t == 0:
+                act[b] = staged("gelu", [P, PACK, KP], F32, bufs=2)
+            nc.scalar.activation(out=act[b][:, t, :], in_=z_bank[b, t][:], func=ACT.Gelu_apprx_tanh)
 
-        def sum_u(s):
-            u_bank[s] = bank()
-            first_stage(u_bank[s], "gate", s)
-
-        def gelu(s):
-            act[s] = staged("gelu", [P, KP], F32)
-            nc.scalar.activation(
-                out=act[s][:].rearrange("p (r t) -> p r t", t=PACK),
-                in_=z_bank[s][:].rearrange("p (t r) -> p r t", t=PACK),
-                func=ACT.Gelu_apprx_tanh,
-            )
-
-        def gate(s):
+        def gate(b, i):
             h = staged("h_grouped", [P, KP], BF16)
             nc.vector.tensor_tensor(
-                out=h[:].rearrange("p (r t) -> p r t", t=PACK),
-                in0=act[s][:].rearrange("p (r t) -> p r t", t=PACK),
-                in1=u_bank[s][:].rearrange("p (t r) -> p r t", t=PACK),
+                out=h[:].rearrange("p (r e t) -> p r t e", t=PACK, e=2),
+                in0=act[b][:, :, i * P : (i + 1) * P].rearrange("p t (r e) -> p r t e", e=2),
+                in1=u_bank[b, i][:].rearrange("p (t r e) -> p r t e", t=PACK, e=2),
                 op=ALU.mult,
             )
-            grouped[("h", s, 0)] = h
+            grouped[("h", b, i)] = h
 
         y = [kept("y%d" % h, [P, PACK, N], F32) for h in range(2)]
         y_grouped = [kept("y_grouped%d" % h, [P, PACK * N], BF16) for h in range(2)]
@@ -255,22 +272,24 @@ def tile_gated_memory_expert_b10_kernel(
         def scale_bias(i):
             nc.scalar.activation(out=y[i // PACK][:, i % PACK, :], in_=bias[:], func=ACT.Copy, scale=gain[:, i : i + 1])
 
-        def down(i):
-            y_bank[i] = bank()
+        def down(i, c0=0, c1=N):
+            y_bank[i, c0] = bank()
             for g in range(GROUPS):
-                hc, hs = operand(("h", g * TILES + i, 0), 0, P)
-                wc, ws = operand(("down", g, 0), 0, N)
+                hc, hs = operand(("h", 2 * g + i // PACK, i % PACK), 0, P)
+                wc, ws = operand(("down", g, 0), c0, c1 - c0)
                 nc.tensor.matmul_mx(
-                    out=y_bank[i][:], lhsT=hc, lhsT_scale=hs, rhs=wc, rhs_scale=ws, start=(g == 0), stop=(g == GROUPS - 1)
+                    out=y_bank[i, c0][:, 0 : c1 - c0], lhsT=hc, lhsT_scale=hs, rhs=wc, rhs_scale=ws,
+                    start=(g == 0), stop=(g == GROUPS - 1),
                 )
 
-        def finish(i):
+        def finish(i, c0=0, c1=N):
             half, t = divmod(i, PACK)
             nc.vector.scalar_tensor_tensor(
-                out=y[half][:, t, :], in0=y_bank[i][:], scalar=gain[:, i : i + 1], in1=y[half][:, t, :],
+                out=y[half][:, t, c0:c1], in0=y_bank[i, c0][:, 0 : c1 - c0], scalar=gain[:, i : i + 1], in1=y[half][:, t, c0:c1],
                 op0=ALU.mult, op1=ALU.add,
             )
-            nc.sync.dma_start(out=y_rows[half, t], in_=y[half][:, t, :])
+            if c1 == N:
+                nc.sync.dma_start(out=y_rows[half, t], in_=y[half][:, t, :])
 
         def interleave_y(engine, half, c0, c1):
             dst = y_grouped[half][:].rearrange("p (c e t) -> p c t e", e=4, t=4)[:, c0 // 4 : c1 // 4, :, :]
@@ -296,98 +315,151 @@ def tile_gated_memory_expert_b10_kernel(
                     out=out_2[half, 4 * q : 4 * q + 4, :].bitcast(I32), in_=y_scales[half][32 * q : 32 * q + 4, :].bitcast(I32)
                 )
 
-        def share(key):
-            interleave("vector", key, 0)
-            interleave("vector", key, 1)
-            interleave("scalar", key, 2)
-            interleave("scalar", key, 3)
+        def share(key, on_vector):
+            for t in range(PACK):
+                interleave("vector" if t < on_vector else "scalar", key, t)
 
-        widen(0)
-        widen(1)
-        turn_x(0)
-        turn_x(1)
-        turn_mem(0)
-        empty(("x", 0, 0))
-        share(("in", 0, 0))
+        units = [(0, 0), (0, 1), (1, 0), (1, 1)]
+        widen(0, 0, 0)
+        widen_plain(0, 1, 0)
+        turn_x(0, 0, 0)
+        widen(0, 0, 1)
+        turn_x(0, 0, 1)
+        widen(0, 1, 1)
+        turn_x(0, 1, 0)
+        empty(("x", 0, 0), 0)
+        empty(("x", 0, 0), 1)
+        share(("in", 0, 0), 3)
+        turn_x(0, 1, 1)
+        turn_mem(0, 0)
+        turn_mem(0, 1)
         quantise(("x", 0, 0))
-        empty(("x", 1, 0))
-        share(("in", 0, 1))
+        empty(("x", 0, 1), 0)
+        empty(("x", 0, 1), 1)
         quantise(("in", 0, 0))
-        empty(("mem", 0, 0))
+        share(("in", 0, 1), 3)
+        empty(("mem", 0, 0), 0)
+        empty(("mem", 0, 0), 1)
         sort_wm(0, 1)
+        quantise(("x", 0, 1))
         sort_wms()
-        quantise(("x", 1, 0))
         quantise(("in", 0, 1))
         quantise(("mem", 0, 0))
-        widen(2)
-        share(("gate", 0, 0))
-        widen(3)
-        share(("gate", 0, 1))
+        share(("gate", 0, 0), 2)
+        for which in (0, 1, "mem"):
+            for t in range(PACK):
+                z_pass(0, t, which, which == 0, which == "mem")
+        share(("gate", 0, 1), 2)
+        for t in range(PACK):
+            gelu(0, t)
         quantise(("gate", 0, 0))
+        widen(1, 0, 0)
         quantise(("gate", 0, 1))
+        widen(1, 0, 1)
+        turn_mem(1, 0)
+        turn_mem(1, 1)
+        empty(("mem", 1, 0), 0)
+        empty(("mem", 1, 0), 1)
 
         quarters = [(key, t) for key in later for t in range(PACK)]
         full = []
-        for s in range(STEPS):
-            ready, full = full, []
-            if s > 0:
-                gate(s - 1)
-            if s > DOWN_FROM:
-                finish(s - 1 - DOWN_FROM)
-            for key in ready:
-                quantise(key)
-            if 1 <= s and s + 1 < TILES:
-                quantise(("x", s + 1, 0))
-                if s % 2 == 1:
-                    quantise(("mem", (s + 1) // 2, 0))
-            sum_z(s)
-            gelu(s)
-            if s % 2 == 0 and s + 2 < TILES:
-                turn_x(s + 2)
-                turn_mem((s + 2) // 2)
-                turn_x(s + 3)
-            sum_u(s)
-            if s + 2 < TILES:
-                empty(("x", s + 2, 0))
-                if s % 2 == 0:
-                    empty(("mem", (s + 2) // 2, 0))
-            if s + 4 < TILES:
-                widen(s + 4)
-            if s == 5:
+
+        def take(engine):
+            if quarters:
+                key, t = quarters.pop(0)
+                interleave(engine, key, t)
+                if t == PACK - 1:
+                    full.append(key)
+
+        for i in range(PACK):
+            sum_u(0, i)
+            c, pair = units[i]
+            turn_x(1, c, pair)
+            empty(("x", 1, c), pair)
+            gate(0, i)
+            if i < 2:
+                widen(1, 1, i)
+            elif i == 2:
+                quantise(("x", 1, 0))
+                quantise(("mem", 1, 0))
+            else:
+                quantise(("x", 1, 1))
+            if i > 0:
+                quantise(("h", 0, i - 1))
+                take("scalar")
+        take("scalar")
+
+        last = BLOCKS - 1
+        for b in range(1, BLOCKS):
+            if b == 1:
+                for which in (0, "mem", 1):
+                    for t in range(PACK):
+                        z_pass(1, t, which, which == 0, which == 1)
                 sort_wm(1, 3)
-            if s == 16:
+            if b == last - 1:
                 nc.vector.tensor_copy(out=gain[:], in_=gain_raw[:].rearrange("p h t -> p (h t)"))
-            on_vector = 0 if s < 4 else (2 if s < TILES else 1)
-            on_scalar = 2 if s in (6, 7) or (s > TILES and s % 2 == 1) else 1
-            for engine, count in (("vector", on_vector), ("scalar", on_scalar)):
-                taken, quarters = quarters[:count], quarters[count:]
-                for key, t in taken:
-                    interleave(engine, key, t)
-                    if t == PACK - 1:
-                        full.append(key)
-            if s > 0:
-                quantise(("h", s - 1, 0))
-            if 18 <= s < 22:
-                scale_bias(2 * (s - 18))
-                scale_bias(2 * (s - 18) + 1)
-            if s >= DOWN_FROM:
-                down(s - DOWN_FROM)
-        last = STEPS - 1
+            if b > 1:
+                gate(b - 1, PACK - 1)
+            for t in range(PACK):
+                while full:
+                    quantise(full.pop(0))
+                if b > 1:
+                    sum_z(b, t)
+                if t == 0:
+                    if b < last:
+                        take("scalar")
+                    else:
+                        scale_bias(0)
+                gelu(b, t)
+                take("vector")
+                if t == 0:
+                    quantise(("h", b - 1, PACK - 1))
+            if b < last:
+                for i in range(PACK):
+                    sum_u(b, i)
+                    if i == 0:
+                        while full:
+                            quantise(full.pop(0))
+                    take("scalar")
+                    if i < PACK - 1:
+                        gate(b, i)
+                    if 0 < i:
+                        quantise(("h", b, i - 1))
+        while full:
+            quantise(full.pop(0))
+        for i in range(1, TILES):
+            scale_bias(i)
+        for i in range(PACK - 1):
+            sum_u(last, i)
+            down(i)
+            gate(last, i)
+            if i > 0:
+                quantise(("h", last, i - 1))
+            finish(i)
+        down(3)
+        sum_u(last, 3)
+        quantise(("h", last, 2))
+        finish(3)
         interleave_y("scalar", 0, 0, 256)
         interleave_y("scalar", 0, 256, 512)
-        gate(last)
+        gate(last, 3)
+        down(4)
         finish(4)
+        quantise(("h", last, 3))
         down(5)
-        quantise(("h", last, 0))
         finish(5)
         down(6)
+        quantise_y(0, 0, 256)
         finish(6)
-        down(7)
-        quantise_y(0, 0, 512)
+        down(7, 0, 256)
+        down(7, 256, 512)
+        quantise_y(0, 256, 512)
         store_scales(0, [nc.sync])
-        finish(7)
+        finish(7, 0, 256)
+        finish(7, 256, 512)
+        interleave_y("scalar", 1, 0, 128)
+        interleave_y("vector", 1, 128, 256)
         interleave_y("scalar", 1, 384, 512)
-        interleave_y("vector", 1, 0, 256)
         interleave_y("vector", 1, 256, 384)
         quantise_y(1, 0, 256)
         quantise_y(1, 256, 512)

@@ -24,6 +24,9 @@ TILES = T // P
 GROUPS = F // KP
 BLOCKS = 2 * GROUPS
 GROUPED_BUFS = 5
+ON_VECTOR = 3
+SCALAR_EARLY = 1
+SCALAR_LATE = 5
 
 
 def tile_gated_memory_expert_b10_kernel(
@@ -125,13 +128,15 @@ def tile_gated_memory_expert_b10_kernel(
 
         wide, turned, grouped, codes, scales = {}, {}, {}, {}, {}
 
-        def quantise(key):
-            src = grouped[key]
-            width = src.shape[1] // PACK
-            name = "%s%d%d" % key
-            codes[key] = kept("codes_" + name, [P, width], U32)
-            scales[key] = kept("scales_" + name, [P, width], U8)
-            nc.vector.quantize_mx(out=codes[key][:].bitcast(FP8X4), scales=scales[key][:], in_=src[:])
+        def quantise(key, first=0, count=KP):
+            if first == 0:
+                name = "%s%d%d" % key
+                codes[key] = kept("codes_" + name, [P, KP], U32)
+                scales[key] = kept("scales_" + name, [P, KP], U8)
+            nc.vector.quantize_mx(
+                out=codes[key][:, first : first + count].bitcast(FP8X4), scales=scales[key][:, first : first + count],
+                in_=grouped[key][:, PACK * first : PACK * (first + count)],
+            )
 
         def fresh_grouped(key):
             grouped[key] = staged("grouped", [P, PACK * KP], BF16, bufs=GROUPED_BUFS)
@@ -186,12 +191,12 @@ def tile_gated_memory_expert_b10_kernel(
                 in_=turned[key, pair][:].rearrange("p (c u r) -> p c r u", c=2, u=2),
             )
 
-        def interleave(engine, key, t):
-            if t == 0:
+        def interleave(engine, key, t0, t1):
+            if t0 == 0:
                 fresh_grouped(key)
-            dst = grouped[key][:].rearrange("p (t a e j) -> p t a j e", t=4, e=4, j=4)[:, t, :, :, :]
+            dst = grouped[key][:].rearrange("p (t a e j) -> p t a j e", t=4, e=4, j=4)[:, t0:t1, :, :, :]
             order = "p j (t a e) -> p t a j e" if key[0] == "down" else "p j (a t e) -> p t a j e"
-            src = raw[key][:].rearrange(order, t=4, e=4)[:, t, :, :, :]
+            src = raw[key][:].rearrange(order, t=4, e=4)[:, t0:t1, :, :, :]
             if engine == "vector":
                 nc.vector.tensor_copy(out=dst, in_=src)
             else:
@@ -253,14 +258,15 @@ def tile_gated_memory_expert_b10_kernel(
             nc.scalar.activation(out=act[b][:, t, :], in_=z_bank[b, t][:], func=ACT.Gelu_apprx_tanh)
 
         def gate(b, i):
-            h = staged("h_grouped", [P, KP], BF16)
+            key = ("h", b, 0)
+            if i == 0:
+                grouped[key] = staged("h_grouped", [P, PACK * KP], BF16, bufs=2)
             nc.vector.tensor_tensor(
-                out=h[:].rearrange("p (r e t) -> p r t e", t=PACK, e=2),
+                out=grouped[key][:, i * KP : (i + 1) * KP].rearrange("p (r e t) -> p r t e", t=PACK, e=2),
                 in0=act[b][:, :, i * P : (i + 1) * P].rearrange("p t (r e) -> p r t e", e=2),
                 in1=u_bank[b, i][:].rearrange("p (t r e) -> p r t e", t=PACK, e=2),
                 op=ALU.mult,
             )
-            grouped[("h", b, i)] = h
 
         y = [kept("y%d" % h, [P, PACK, N], F32) for h in range(2)]
         y_grouped = [kept("y_grouped%d" % h, [P, PACK * N], BF16) for h in range(2)]
@@ -275,7 +281,7 @@ def tile_gated_memory_expert_b10_kernel(
         def down(i, c0=0, c1=N):
             y_bank[i, c0] = bank()
             for g in range(GROUPS):
-                hc, hs = operand(("h", 2 * g + i // PACK, i % PACK), 0, P)
+                hc, hs = operand(("h", 2 * g + i // PACK, 0), (i % PACK) * P, P)
                 wc, ws = operand(("down", g, 0), c0, c1 - c0)
                 nc.tensor.matmul_mx(
                     out=y_bank[i, c0][:, 0 : c1 - c0], lhsT=hc, lhsT_scale=hs, rhs=wc, rhs_scale=ws,
@@ -316,10 +322,11 @@ def tile_gated_memory_expert_b10_kernel(
                 )
 
         def share(key, on_vector):
-            for t in range(PACK):
-                interleave("vector" if t < on_vector else "scalar", key, t)
+            interleave("vector", key, 0, 2)
+            if on_vector == 3:
+                interleave("vector", key, 2, 3)
+            interleave("scalar", key, on_vector, PACK)
 
-        units = [(0, 0), (0, 1), (1, 0), (1, 1)]
         widen(0, 0, 0)
         widen_plain(0, 1, 0)
         turn_x(0, 0, 0)
@@ -364,30 +371,39 @@ def tile_gated_memory_expert_b10_kernel(
         quarters = [(key, t) for key in later for t in range(PACK)]
         full = []
 
-        def take(engine):
-            if quarters:
-                key, t = quarters.pop(0)
-                interleave(engine, key, t)
-                if t == PACK - 1:
+        def take(engine, count):
+            taken = [quarters.pop(0) for n in range(min(count, len(quarters)))]
+            while taken:
+                key, t = taken[0]
+                run = len([1 for other, n in taken if other == key])
+                interleave(engine, key, t, t + run)
+                if t + run == PACK:
                     full.append(key)
+                taken = taken[run:]
+
+        def quantise_full():
+            while full:
+                quantise(full.pop(0))
 
         for i in range(PACK):
             sum_u(0, i)
-            c, pair = units[i]
-            turn_x(1, c, pair)
-            empty(("x", 1, c), pair)
+            if i % 2 == 0:
+                for pair in range(2):
+                    turn_x(1, i // 2, pair)
+                for pair in range(2):
+                    empty(("x", 1, i // 2), pair)
             gate(0, i)
-            if i < 2:
-                widen(1, 1, i)
-            elif i == 2:
+            if i == 0:
+                widen(1, 1, 0)
+                widen(1, 1, 1)
+            elif i == 1:
                 quantise(("x", 1, 0))
+            elif i == 2:
                 quantise(("mem", 1, 0))
             else:
                 quantise(("x", 1, 1))
-            if i > 0:
-                quantise(("h", 0, i - 1))
-                take("scalar")
-        take("scalar")
+            if i % 2 == 1:
+                take("scalar", 2)
 
         last = BLOCKS - 1
         for b in range(1, BLOCKS):
@@ -400,33 +416,26 @@ def tile_gated_memory_expert_b10_kernel(
                 nc.vector.tensor_copy(out=gain[:], in_=gain_raw[:].rearrange("p h t -> p (h t)"))
             if b > 1:
                 gate(b - 1, PACK - 1)
+            quantise_full()
             for t in range(PACK):
-                while full:
-                    quantise(full.pop(0))
                 if b > 1:
                     sum_z(b, t)
                 if t == 0:
                     if b < last:
-                        take("scalar")
+                        take("scalar", 3 if b == 1 else SCALAR_EARLY)
                     else:
                         scale_bias(0)
                 gelu(b, t)
-                take("vector")
-                if t == 0:
-                    quantise(("h", b - 1, PACK - 1))
+            take("vector", 2)
+            take("vector", ON_VECTOR - 2)
+            quantise_full()
+            quantise(("h", b - 1, 0))
             if b < last:
+                take("scalar", SCALAR_LATE)
                 for i in range(PACK):
                     sum_u(b, i)
-                    if i == 0:
-                        while full:
-                            quantise(full.pop(0))
-                    take("scalar")
                     if i < PACK - 1:
                         gate(b, i)
-                    if 0 < i:
-                        quantise(("h", b, i - 1))
-        while full:
-            quantise(full.pop(0))
         for i in range(1, TILES):
             scale_bias(i)
         for i in range(PACK - 1):
@@ -434,18 +443,18 @@ def tile_gated_memory_expert_b10_kernel(
             down(i)
             gate(last, i)
             if i > 0:
-                quantise(("h", last, i - 1))
+                quantise(("h", last, 0), (i - 1) * P, P)
             finish(i)
         down(3)
         sum_u(last, 3)
-        quantise(("h", last, 2))
+        quantise(("h", last, 0), 2 * P, P)
         finish(3)
         interleave_y("scalar", 0, 0, 256)
         interleave_y("scalar", 0, 256, 512)
         gate(last, 3)
         down(4)
         finish(4)
-        quantise(("h", last, 3))
+        quantise(("h", last, 0), 3 * P, P)
         down(5)
         finish(5)
         down(6)

from contextlib import ExitStack

import concourse.mybir as mybir
from concourse.masks import make_identity

T, D, R, F, N = 1024, 1024, 512, 1536, 512
FLOPS = 2 * T * (2 * D * F + R * F + F * N)

F32 = mybir.dt.float32
BF16 = mybir.dt.bfloat16
I32 = mybir.dt.int32
U32 = mybir.dt.uint32
U8 = mybir.dt.uint8
FP8 = mybir.dt.float8_e4m3fn
FP8X4 = mybir.dt.float8_e4m3fn_x4
FP4X4 = mybir.dt.float4_e2m1fn_x4
ACT = mybir.ActivationFunctionType
ALU = mybir.AluOpType

P = 128
PACK = 4
KP = P * PACK
TILES = T // P
GROUPS = F // KP
BLOCKS = 2 * GROUPS
GROUPED_BUFS = 5
ON_VECTOR = 3
SCALAR_EARLY = 1
SCALAR_LATE = 5


def tile_gated_memory_expert_b10_kernel(
    tc, X_bytes, X_scale, mem, w_in, w_gate, w_mem_words, w_mem_scales, w_down, b_down, slot_gain,
    out_0, out_1, out_2,
):
    nc = tc.nc
    with ExitStack() as ctx:
        keep = ctx.enter_context(tc.tile_pool(name="keep", bufs=1))
        stage = ctx.enter_context(tc.tile_pool(name="stage", bufs=3))
        psum = ctx.enter_context(tc.psum_pool(name="psum", bufs=8))
        ctx.enter_context(tc.manual_schedule())

        def kept(name, shape, dtype):
            return keep.tile(shape, dtype, name=name, align_bytes=64)

        def staged(name, shape, dtype, bufs=3):
            return stage.tile(shape, dtype, name=name, tag=name, bufs=bufs, align_bytes=64)

        def bank():
            return psum.tile([P, 512], F32, name="bank", tag="bank")

        x_rows = X_bytes.rearrange("(h p t) k -> h p (t k)", p=P, t=PACK)
        mem_rows = mem.rearrange("(h p t) k -> h p (t k)", p=P, t=PACK)
        x_src, mem_src, raw = {}, {}, {}

        def load_x(first, count):
            half, t = divmod(first, PACK)
            xb = kept("xbytes%d" % first, [P, count * D], U8)
            nc.sync.dma_start(out=xb[:], in_=x_rows[half, :, t * D : (t + count) * D])
            for n in range(count):
                x_src[first + n] = xb[:, n * D : (n + 1) * D]

        def load_mem(pair):
            half, t = divmod(2 * pair, PACK)
            mt = kept("mem%d" % pair, [P, 2 * R], BF16)
            nc.sync.dma_start(out=mt[:], in_=mem_rows[half, :, t * R : (t + 2) * R])
            mem_src[pair] = mt

        def load_w(key):
            which, g, c = key
            rt = kept("raw_%s%d%d" % key, [P, PACK, KP], BF16)
            if which == "down":
                rows = w_down[g * KP : (g + 1) * KP, :].rearrange("(a t e) n -> e a t n", t=PACK, e=PACK)
                for e in range(PACK):
                    nc.sync.dma_start(out=rt[e:P:PACK, :, :], in_=rows[e])
            else:
                w = w_in if which == "in" else w_gate
                rows = w[c * KP : (c + 1) * KP, g * KP : (g + 1) * KP]
                nc.sync.dma_start(out=rt[:], in_=rows.rearrange("(p j) n -> p j n", j=PACK))
            raw[key] = rt

        wm_raw = {}

        def load_wm(g0, g1):
            wt = kept("wm_raw%d" % g0, [P, (g1 - g0) * 2 * KP], U8)
            nc.sync.dma_start(out=wt[:].bitcast(I32), in_=w_mem_words[0, :, g0 * 2 * KP : g1 * 2 * KP].bitcast(I32))
            wm_raw[g0] = wt

        ident = kept("ident", [P, P], F32)
        make_identity(nc, ident[:])
        wms_raw = kept("wms_raw", [P, F], U8)
        nc.vector.memset(wms_raw[:].bitcast(I32), 0)
        warm = kept("warm", [P, 2], F32)
        nc.vector.memset(warm[:, 0:1], 0.0)
        nc.scalar.activation(out=warm[:, 1:2], in_=warm[:, 0:1], func=ACT.Gelu_apprx_tanh)

        xs = kept("xs", [P, 2, PACK * 8], F32)
        load_x(0, 2)
        nc.sync.dma_start(out=xs[:], in_=X_scale.rearrange("(h p t) j -> p h (t j)", p=P, t=PACK))
        load_x(2, 2)
        load_w(("in", 0, 0))
        load_mem(0)
        load_mem(1)
        load_w(("in", 0, 1))
        load_wm(0, 1)
        for q in range(4):
            nc.sync.dma_start(
                out=wms_raw[32 * q : 32 * q + 4, :].bitcast(I32), in_=w_mem_scales[0, 4 * q : 4 * q + 4, :].bitcast(I32)
            )
        load_w(("gate", 0, 0))
        load_w(("gate", 0, 1))
        load_x(4, 4)
        load_mem(2)
        load_mem(3)
        load_w(("in", 1, 0))
        load_w(("in", 1, 1))
        load_wm(1, 3)
        later = [("in", 1, 0), ("in", 1, 1), ("gate", 1, 0), ("gate", 1, 1)]
        later = later + [("in", 2, 0), ("in", 2, 1), ("gate", 2, 0), ("gate", 2, 1)]
        later = later + [("down", g, 0) for g in range(GROUPS)]
        for key in later[2:]:
            load_w(key)
        bias = kept("bias", [P, N], BF16)
        nc.sync.dma_start(out=bias[:], in_=b_down.rearrange("o n -> (o n)").partition_broadcast(P))
        gain_raw = kept("gain_raw", [P, 2, PACK], BF16)
        nc.sync.dma_start(out=gain_raw[:], in_=slot_gain.rearrange("(h p t) o -> p h (t o)", p=P, t=PACK))
        gain = kept("gain", [P, TILES], F32)

        wide, turned, grouped, codes, scales = {}, {}, {}, {}, {}

        def quantise(key, first=0, count=KP):
            if first == 0:
                name = "%s%d%d" % key
                codes[key] = kept("codes_" + name, [P, KP], U32)
                scales[key] = kept("scales_" + name, [P, KP], U8)
            nc.vector.quantize_mx(
                out=codes[key][:, first : first + count].bitcast(FP8X4), scales=scales[key][:, first : first + count],
                in_=grouped[key][:, PACK * first : PACK * (first + count)],
            )

        def fresh_grouped(key):
            grouped[key] = staged("grouped", [P, PACK * KP], BF16, bufs=GROUPED_BUFS)

        def widen_plain(half, c, pair):
            xw = staged("xw", [P, 2 * KP], BF16, bufs=4)
            for n in range(2):
                for q in range(4):
                    t = 2 * pair + n
                    b = 4 * c + q
                    nc.scalar.activation(
                        out=xw[:, n * KP + q * P : n * KP + (q + 1) * P], in_=x_src[PACK * half + t][:, b * P : (b + 1) * P].bitcast(FP8),
                        func=ACT.Copy, scale=xs[:, half, t * 8 + b : t * 8 + b + 1],
                    )
            words = xw[:].bitcast(F32)
            wide[(half, c, pair)] = [words[:, 256 * n + u : 256 * (n + 1) : 2] for n in range(2) for u in range(2)]

        def widen(half, c, pair):
            xw = staged("xw", [P, 2 * KP], BF16, bufs=4)
            dst = xw[:].rearrange("p (n u q r e) -> p n q r u e", n=2, u=2, q=4, e=2)
            for q in range(4):
                for n in range(2):
                    t = 2 * pair + n
                    b = 4 * c + q
                    src = x_src[PACK * half + t][:, b * P : (b + 1) * P].bitcast(FP8).rearrange("p (r u e) -> p r u e", u=2, e=2)
                    nc.vector.tensor_scalar(
                        out=dst[:, n, q, :, :, :], in0=src, scalar1=xs[:, half, t * 8 + b : t * 8 + b + 1], scalar2=None,
                        op0=ALU.mult,
                    )
            words = xw[:].bitcast(F32)
            wide[(half, c, pair)] = [words[:, n * P : (n + 1) * P] for n in range(4)]

        def turn_x(half, c, pair):
            pt = bank()
            for n in range(4):
                nc.tensor.transpose(pt[:, n * P : (n + 1) * P], wide[(half, c, pair)][n], ident[:])
            turned[("x", half, c), pair] = pt

        def turn_mem(half, pair):
            words = mem_src[2 * half + pair][:].bitcast(F32)
            pt = bank()
            for n in range(4):
                c, u = divmod(n, 2)
                nc.tensor.transpose(pt[:, n * P : (n + 1) * P], words[:, 256 * c + u : 256 * (c + 1) : 2], ident[:])
            turned[("mem", half, 0), pair] = pt

        def empty(key, pair):
            if pair == 0:
                fresh_grouped(key)
            nc.scalar.copy(
                out=grouped[key][:, pair * 2 * KP : (pair + 1) * 2 * KP].bitcast(F32).rearrange("p (c r u) -> p c r u", c=2, u=2),
                in_=turned[key, pair][:].rearrange("p (c u r) -> p c r u", c=2, u=2),
            )

        def interleave(engine, key, t0, t1):
            if t0 == 0:
                fresh_grouped(key)
            dst = grouped[key][:].rearrange("p (t a e j) -> p t a j e", t=4, e=4, j=4)[:, t0:t1, :, :, :]
            order = "p j (t a e) -> p t a j e" if key[0] == "down" else "p j (a t e) -> p t a j e"
            src = raw[key][:].rearrange(order, t=4, e=4)[:, t0:t1, :, :, :]
            if engine == "vector":
                nc.vector.tensor_copy(out=dst, in_=src)
            else:
                nc.scalar.copy(out=dst, in_=src)

        wm = kept("wm", [P, GROUPS * 2 * KP], U8)
        wms = kept("wms", [P, F], U8)

        def sort_wm(g0, g1):
            nc.vector.tensor_copy(
                out=wm[:, g0 * 2 * KP : g1 * 2 * KP].bitcast(I32).rearrange("p (g t a w) -> p g t a w", t=4, a=32, w=2),
                in_=wm_raw[g0][:].bitcast(I32).rearrange("p (g a t w) -> p g t a w", t=4, a=32, w=2),
            )

        def sort_wms():
            nc.vector.tensor_copy(
                out=wms[:].bitcast(I32).rearrange("p (g t a) -> p g t a", t=4, a=32),
                in_=wms_raw[:].bitcast(I32).rearrange("p (g a t) -> p g t a", t=4, a=32),
            )

        def operand(key, first, count):
            return codes[key][:, first : first + count].bitcast(FP8X4), scales[key][:, first : first + count]

        z_bank, u_bank, act = {}, {}, {}

        def z_pass(b, t, which, start, stop):
            g, half = divmod(b, 2)
            if start:
                z_bank[b, t] = bank()
            if which == "mem":
                col = g * KP + t * P
                wc, ws = wm[:, 2 * col : 2 * (col + P)].bitcast(FP4X4), wms[:, col : col + P]
                xc, xsc = operand(("mem", half, 0), 0, KP)
            else:
                wc, ws = operand(("in", g, which), t * P, P)
                xc, xsc = operand(("x", half, which), 0, KP)
            nc.tensor.matmul_mx(out=z_bank[b, t][:], lhsT=wc, lhsT_scale=ws, rhs=xc, rhs_scale=xsc, start=start, stop=stop)

        def sum_z(b, t):
            z_pass(b, t, 0, True, False)
            z_pass(b, t, "mem", False, False)
            z_pass(b, t, 1, False, True)

        def sum_u(b, i):
            g, half = divmod(b, 2)
            u_bank[b, i] = bank()
            for t in range(PACK):
                for c in range(2):
                    wc, ws = operand(("gate", g, c), t * P, P)
                    xc, xsc = operand(("x", half, c), i * P, P)
                    nc.tensor.matmul_mx(
                        out=u_bank[b, i][:, t * P : (t + 1) * P], lhsT=wc, lhsT_scale=ws, rhs=xc, rhs_scale=xsc,
                        start=(c == 0), stop=(c == 1),
                    )

        def gelu(b, t):
            if t == 0:
                act[b] = staged("gelu", [P, PACK, KP], F32, bufs=2)
            nc.scalar.activation(out=act[b][:, t, :], in_=z_bank[b, t][:], func=ACT.Gelu_apprx_tanh)

        def gate(b, i):
            key = ("h", b, 0)
            if i == 0:
                grouped[key] = staged("h_grouped", [P, PACK * KP], BF16, bufs=2)
            nc.vector.tensor_tensor(
                out=grouped[key][:, i * KP : (i + 1) * KP].rearrange("p (r e t) -> p r t e", t=PACK, e=2),
                in0=act[b][:, :, i * P : (i + 1) * P].rearrange("p t (r e) -> p r t e", e=2),
                in1=u_bank[b, i][:].rearrange("p (t r e) -> p r t e", t=PACK, e=2),
                op=ALU.mult,
            )

        y = [kept("y%d" % h, [P, PACK, N], F32) for h in range(2)]
        y_grouped = [kept("y_grouped%d" % h, [P, PACK * N], BF16) for h in range(2)]
        y_codes = [kept("y_codes%d" % h, [P, N], U32) for h in range(2)]
        y_scales = [kept("y_scales%d" % h, [P, N], U8) for h in range(2)]
        y_rows = out_0.rearrange("(h p t) n -> h t p n", p=P, t=PACK)
        y_bank = {}

        def scale_bias(i):
            nc.scalar.activation(out=y[i // PACK][:, i % PACK, :], in_=bias[:], func=ACT.Copy, scale=gain[:, i : i + 1])

        def down(i, c0=0, c1=N):
            y_bank[i, c0] = bank()
            for g in range(GROUPS):
                hc, hs = operand(("h", 2 * g + i // PACK, 0), (i % PACK) * P, P)
                wc, ws = operand(("down", g, 0), c0, c1 - c0)
                nc.tensor.matmul_mx(
                    out=y_bank[i, c0][:, 0 : c1 - c0], lhsT=hc, lhsT_scale=hs, rhs=wc, rhs_scale=ws,
                    start=(g == 0), stop=(g == GROUPS - 1),
                )

        def finish(i, c0=0, c1=N):
            half, t = divmod(i, PACK)
            nc.vector.scalar_tensor_tensor(
                out=y[half][:, t, c0:c1], in0=y_bank[i, c0][:, 0 : c1 - c0], scalar=gain[:, i : i + 1], in1=y[half][:, t, c0:c1],
                op0=ALU.mult, op1=ALU.add,
            )
            if c1 == N:
                nc.sync.dma_start(out=y_rows[half, t], in_=y[half][:, t, :])

        def interleave_y(engine, half, c0, c1):
            dst = y_grouped[half][:].rearrange("p (c e t) -> p c t e", e=4, t=4)[:, c0 // 4 : c1 // 4, :, :]
            src = y[half][:].rearrange("p t (c e) -> p c t e", e=4)[:, c0 // 4 : c1 // 4, :, :]
            if engine == "vector":
                nc.vector.tensor_copy(out=dst, in_=src)
            else:
                nc.scalar.copy(out=dst, in_=src)

        def quantise_y(half, c0, c1):
            nc.vector.quantize_mx(
                out=y_codes[half][:, c0:c1].bitcast(FP8X4), scales=y_scales[half][:, c0:c1],
                in_=y_grouped[half][:, PACK * c0 : PACK * c1],
            )
            nc.sync.dma_start(
                out=out_1[half].rearrange("p m t -> p (m t)")[:, PACK * c0 : PACK * c1].bitcast(I32),
                in_=y_codes[half][:, c0:c1].bitcast(I32),
            )

        def store_scales(half, queues):
            for q in range(4):
                queues[q % len(queues)].dma_start(
                    out=out_2[half, 4 * q : 4 * q + 4, :].bitcast(I32), in_=y_scales[half][32 * q : 32 * q + 4, :].bitcast(I32)
                )

        def share(key, on_vector):
            interleave("vector", key, 0, 2)
            if on_vector == 3:
                interleave("vector", key, 2, 3)
            interleave("scalar", key, on_vector, PACK)

        widen(0, 0, 0)
        widen_plain(0, 1, 0)
        turn_x(0, 0, 0)
        widen(0, 0, 1)
        turn_x(0, 0, 1)
        widen(0, 1, 1)
        turn_x(0, 1, 0)
        empty(("x", 0, 0), 0)
        empty(("x", 0, 0), 1)
        share(("in", 0, 0), 3)
        turn_x(0, 1, 1)
        turn_mem(0, 0)
        turn_mem(0, 1)
        quantise(("x", 0, 0))
        empty(("x", 0, 1), 0)
        empty(("x", 0, 1), 1)
        quantise(("in", 0, 0))
        share(("in", 0, 1), 3)
        empty(("mem", 0, 0), 0)
        empty(("mem", 0, 0), 1)
        sort_wm(0, 1)
        quantise(("x", 0, 1))
        sort_wms()
        quantise(("in", 0, 1))
        quantise(("mem", 0, 0))
        share(("gate", 0, 0), 2)
        for which in (0, 1, "mem"):
            for t in range(PACK):
                z_pass(0, t, which, which == 0, which == "mem")
        share(("gate", 0, 1), 2)
        for t in range(PACK):
            gelu(0, t)
        quantise(("gate", 0, 0))
        widen(1, 0, 0)
        quantise(("gate", 0, 1))
        widen(1, 0, 1)
        turn_mem(1, 0)
        turn_mem(1, 1)
        empty(("mem", 1, 0), 0)
        empty(("mem", 1, 0), 1)

        quarters = [(key, t) for key in later for t in range(PACK)]
        full = []

        def take(engine, count):
            taken = [quarters.pop(0) for n in range(min(count, len(quarters)))]
            while taken:
                key, t = taken[0]
                run = len([1 for other, n in taken if other == key])
                interleave(engine, key, t, t + run)
                if t + run == PACK:
                    full.append(key)
                taken = taken[run:]

        def quantise_full():
            while full:
                quantise(full.pop(0))

        for i in range(PACK):
            sum_u(0, i)
            if i % 2 == 0:
                for pair in range(2):
                    turn_x(1, i // 2, pair)
                for pair in range(2):
                    empty(("x", 1, i // 2), pair)
            gate(0, i)
            if i == 0:
                widen(1, 1, 0)
                widen(1, 1, 1)
            elif i == 1:
                quantise(("x", 1, 0))
            elif i == 2:
                quantise(("mem", 1, 0))
            else:
                quantise(("x", 1, 1))
            if i % 2 == 1:
                take("scalar", 2)

        last = BLOCKS - 1
        for b in range(1, BLOCKS):
            if b == 1:
                for which in (0, "mem", 1):
                    for t in range(PACK):
                        z_pass(1, t, which, which == 0, which == 1)
                sort_wm(1, 3)
            if b == last - 1:
                nc.vector.tensor_copy(out=gain[:], in_=gain_raw[:].rearrange("p h t -> p (h t)"))
            if b > 1:
                gate(b - 1, PACK - 1)
            quantise_full()
            for t in range(PACK):
                if b > 1:
                    sum_z(b, t)
                if t == 0:
                    if b < last:
                        take("scalar", 3 if b == 1 else SCALAR_EARLY)
                    else:
                        scale_bias(0)
                gelu(b, t)
            take("vector", 2)
            take("vector", ON_VECTOR - 2)
            quantise_full()
            quantise(("h", b - 1, 0))
            if b < last:
                take("scalar", SCALAR_LATE)
                for i in range(PACK):
                    sum_u(b, i)
                    if i < PACK - 1:
                        gate(b, i)
        for i in range(1, TILES):
            scale_bias(i)
        for i in range(PACK - 1):
            sum_u(last, i)
            down(i)
            gate(last, i)
            if i > 0:
                quantise(("h", last, 0), (i - 1) * P, P)
            finish(i)
        down(3)
        sum_u(last, 3)
        quantise(("h", last, 0), 2 * P, P)
        finish(3)
        interleave_y("scalar", 0, 0, 256)
        interleave_y("scalar", 0, 256, 512)
        gate(last, 3)
        down(4)
        finish(4)
        quantise(("h", last, 0), 3 * P, P)
        down(5)
        finish(5)
        down(6)
        quantise_y(0, 0, 256)
        finish(6)
        down(7, 0, 256)
        down(7, 256, 512)
        quantise_y(0, 256, 512)
        store_scales(0, [nc.sync])
        finish(7, 0, 256)
        finish(7, 256, 512)
        interleave_y("scalar", 1, 0, 128)
        interleave_y("vector", 1, 128, 256)
        interleave_y("scalar", 1, 384, 512)
        interleave_y("vector", 1, 256, 384)
        quantise_y(1, 0, 256)
        quantise_y(1, 256, 512)
        store_scales(1, [nc.scalar, nc.sync])
